import numpy as np
import ml_dtypes


def mxq(x, axis, fmt="e4m3"):
    dtype, down = {"e4m3": (ml_dtypes.float8_e4m3fn, 7), "e5m2": (ml_dtypes.float8_e5m2, 14)}[fmt]
    v = np.moveaxis(np.asarray(x, np.float32).astype(ml_dtypes.bfloat16).astype(np.float64), axis, -1)
    blocks = v.reshape(v.shape[:-1] + (-1, 32))
    amax = np.abs(blocks).max(-1, keepdims=True)
    byte = np.maximum(np.where(amax > 0, np.frexp(amax)[1] - 1 + 127, 0) - down, 1)
    scale = np.exp2(byte - 127.0)
    codes = (blocks / scale).astype(np.float32).astype(dtype).astype(np.float64)
    return np.moveaxis((codes * scale).reshape(v.shape), -1, axis)


WIDE = False


def mx_kscale(k):
    if not WIDE:
        return np.ones(k)
    levels = np.array([10, -10, 5, -5, 0])
    if k % 512:
        return np.exp2(np.random.permutation(np.resize(levels, k // 32))).repeat(32)
    a = np.empty((k // 512, 16))
    for p in range(k // 512):
        a[p, :8] = np.random.permutation(np.resize(levels, 8))
        for g in range(8):
            far = levels[np.abs(levels - a[p, g]) >= 10]
            a[p, g + 8] = far[np.random.randint(len(far))]
    return np.exp2(a.ravel()).repeat(32)


def f64(x):
    return np.asarray(x).astype(np.float64)


def striped(idx):
    return np.tile(idx.reshape(-1, 16).T, (8, 1)).astype(np.uint16)


def unstriped(offs):
    return offs[:16].T.reshape(-1).astype(np.int64)


E2M1 = np.array([0.0, 0.5, 1.0, 1.5, 2.0, 3.0, 4.0, 6.0, -0.0, -0.5, -1.0, -1.5, -2.0, -3.0, -4.0, -6.0])


def pack_weight(w, fmt):
    k, n = w.shape
    w = f64(np.asarray(w, np.float32).astype(ml_dtypes.bfloat16)).reshape(k // 32, 32, n)
    amax = np.abs(w).max(1)
    if fmt == "e4m3":
        byte = np.frexp(amax)[1] - 1 + 127 - 7
    else:
        mant, ex = np.frexp(amax / 6.0)
        byte = np.where(mant > 0.5, ex, ex - 1) + 127
    byte = np.clip(np.where(amax > 0, byte, 1), 1, 254)
    scaled = (w * np.exp2(127.0 - byte)[:, None, :]).reshape(k, n).astype(np.float32)
    by_word = np.ascontiguousarray(scaled.reshape(k // 512, 128, 4, n).transpose(0, 1, 3, 2))
    if fmt == "e4m3":
        words = by_word.astype(ml_dtypes.float8_e4m3fn).view(np.uint8)
    else:
        c = by_word.astype(ml_dtypes.float4_e2m1fn).view(np.uint8) & 0xF
        words = (c[..., 0::2] | (c[..., 1::2] << 4)).reshape(k // 512, 128, 2 * n)
    return np.ascontiguousarray(words), np.ascontiguousarray(byte.astype(np.uint8).reshape(k // 512, 16, n))


def unpack_weight(words, scales, fmt):
    g, _, n = scales.shape
    words = np.ascontiguousarray(words).reshape(g, 128, n, -1)
    if fmt == "e4m3":
        vals = words.view(ml_dtypes.float8_e4m3fn).astype(np.float64)
    else:
        nib = np.empty((g, 128, n, 4), np.uint8)
        nib[..., 0::2] = words & 0xF
        nib[..., 1::2] = words >> 4
        vals = E2M1[nib]
    vals = vals * np.repeat(np.exp2(scales.astype(np.float64) - 127.0), 8, axis=1)[..., None]
    return vals.transpose(0, 1, 3, 2).reshape(g * 512, n)


def relu2(v):
    return np.maximum(v, 0.0) ** 2


K, T, E, C, N = 1536, 512, 8, 128, 256


def by_expert(wq, xq):
    return np.concatenate([wq[e].T @ xq[:, e * C:(e + 1) * C] for e in range(E)], axis=1)


def setup_inputs():
    n = np.random.standard_normal
    s = mx_kscale(K)[:, None]
    first = np.random.permutation(np.repeat(np.arange(E), T // E))
    second = (first + 1 + np.random.permutation(np.repeat(np.arange(E - 1), -(-T // (E - 1)))[:T])) % E
    while np.bincount(second, minlength=E).max() != T // E:
        load = np.bincount(second, minlength=E); hi, lo = int(load.argmax()), int(load.argmin())
        t = np.flatnonzero((second == hi) & (first != lo))[0]; second[t] = lo
    slot_token = np.empty(E * C, np.int64); pos = np.empty((2, T), np.int64); fill = np.zeros(E, np.int64)
    place = np.stack([np.random.permutation(C) for _ in range(E)])
    for r, deal in enumerate((first, second)):
        for t in np.random.permutation(T):
            e = deal[t]; j = e * C + place[e, fill[e]]; fill[e] += 1; slot_token[j] = t; pos[r, t] = j
    g = np.random.uniform(0.2, 0.8, T)
    w = [pack_weight(m, "e2m1") for m in n((E, K, N)) / np.sqrt(K) / s[None]]
    w_slot = np.empty(E * C); w_slot[pos[0]] = g; w_slot[pos[1]] = 1.0 - g
    return {
        "xT": (n((K, T)) * s).astype(np.float32),
        "w_words": np.stack([m[0] for m in w]),
        "w_scales": np.stack([m[1] for m in w]),
        "b": (0.3 * n((N, E))).astype(np.float32),
        "gate": np.tile(w_slot, (K, 1)).astype(np.float32),
        "offs": striped(slot_token),
        "pos1": striped(pos[0]),
        "pos2": striped(pos[1]),
    }


def reference(xT, w_words, w_scales, b, gate, offs, pos1, pos2):
    idx = unstriped(offs)
    w = np.stack([unpack_weight(w_words[e], w_scales[e], "e2m1") for e in range(E)])
    xq = mxq(f64(gate) * f64(xT)[:, idx], 0, "e4m3")
    y = by_expert(w, xq)
    y = relu2(y + np.repeat(f64(b), C, axis=1))
    return y[:, unstriped(pos1)] + y[:, unstriped(pos2)]

@@ -1,0 +1,168 @@
+from contextlib import ExitStack
+
+import concourse.mybir as mybir
+
+K, T, E, C, N = 1536, 512, 8, 128, 256
+S = E * C
+FLOPS = 2 * K * N * S
+
+F32 = mybir.dt.float32
+BF16 = mybir.dt.bfloat16
+I32 = mybir.dt.int32
+U32 = mybir.dt.uint32
+U16 = mybir.dt.uint16
+U8 = mybir.dt.uint8
+FP8X4 = mybir.dt.float8_e4m3fn_x4
+FP4X4 = mybir.dt.float4_e2m1fn_x4
+ALU = mybir.AluOpType
+ACT = mybir.ActivationFunctionType
+
+P = 128
+PACK = 4
+PASSES = K // (P * PACK)
+HALVES = N // P
+PAIR = 2 * C
+
+
+def tile_moe_pre_lin_relu2_kernel(tc, xT, w_words, w_scales, b, gate, offs, pos1, pos2, out):
+    nc = tc.nc
+    with ExitStack() as ctx:
+        keep = ctx.enter_context(tc.tile_pool(name="keep", bufs=1))
+        ring = ctx.enter_context(tc.tile_pool(name="ring", bufs=2))
+        psum = ctx.enter_context(tc.psum_pool(name="psum", bufs=1))
+
+        offs_t = keep.tile([P, S // 16], U16, name="offs_t")
+        pos1_t = keep.tile([P, T // 16], U16, name="pos1_t")
+        pos2_t = keep.tile([P, T // 16], U16, name="pos2_t")
+        gate_a = keep.tile([P, PAIR], F32, name="gate_a")
+        gate_b = keep.tile([P, S - PAIR], F32, name="gate_b")
+        x = [[keep.tile([P, T], F32, name="x%d%d" % (a, j)) for j in range(PACK)] for a in range(PASSES)]
+        w_plane = keep.tile([P, E * PASSES, N], U8, name="w_plane", align_bytes=64)
+        w = [keep.tile([P, 2 * PASSES, 2 * N], U8, name="w%d" % g, align_bytes=64) for g in range(E // 2)]
+        bias = keep.tile([P, HALVES, E], F32, name="bias")
+        y = [keep.tile([P, S], F32, name="y%d" % h) for h in range(HALVES)]
+        warm = keep.tile([P, 8], F32, name="warm")
+        warm2 = keep.tile([P, 8], F32, name="warm2")
+
+        def x_rows(a, j):
+            return xT[a * P * PACK:(a + 1) * P * PACK, :].rearrange("(p j) t -> p j t", j=PACK)[:, j, :]
+
+        nc.vector.memset(w_plane[:].rearrange("p g n -> p (g n)").bitcast(I32), 0)
+        nc.vector.memset(warm[:], 0.0)
+        nc.scalar.dma_start(out=gate_a[:], in_=gate[0:P, 0:PAIR])
+        nc.sync.dma_start(offs_t[:], offs)
+        nc.sync.dma_start(out=x[0][0][:], in_=x_rows(0, 0))
+        nc.sync.dma_start(out=gate_b[:], in_=gate[0:P, PAIR:S])
+        nc.scalar.activation(warm2[:], warm[:], ACT.Relu)
+        for a in range(PASSES):
+            for j in range(PACK):
+                if (a, j) != (0, 0):
+                    nc.sync.dma_start(out=x[a][j][:], in_=x_rows(a, j))
+        scales = w_scales.bitcast(I32).rearrange("e a q n -> q (e a) n")
+        for q in range(4):
+            nc.sync.dma_start(out=w_plane[32 * q:32 * q + 4, :, :].bitcast(I32), in_=scales[4 * q:4 * q + 4])
+        words = w_words.bitcast(I32).rearrange("e a p n -> p (e a) n")
+        for g in range(E // 2):
+            nc.sync.dma_start(out=w[g][:].bitcast(I32), in_=words[:, 2 * PASSES * g:2 * PASSES * (g + 1), :])
+        nc.sync.dma_start(out=bias[:], in_=b.rearrange("(h p) e -> p h e", p=P))
+        nc.sync.dma_start(pos1_t[:], pos1)
+        nc.sync.dma_start(pos2_t[:], pos2)
+
+        def gate_cols(s0, n):
+            return gate_a[:, s0:s0 + n] if s0 < PAIR else gate_b[:, s0 - PAIR:s0 - PAIR + n]
+
+        def gather(dst, a, j, s0, n):
+            window = x[a][j][:].indirect(offs_t[:, s0 // 16:(s0 + n) // 16])
+            nc.vector.tensor_tensor(dst[:, j, :], window, gate_cols(s0, n), ALU.mult)
+
+        codes = {}
+
+        stage = [keep.tile([P, 2 * PAIR], F32, name="stage%d" % i, align_bytes=64) for i in range(3)]
+
+        def weave(src, n, buf, on_vector=False):
+            woven = buf[:].bitcast(BF16)[:, 0:n * PACK]
+            dst = woven.rearrange("p (s j) -> p s j", j=PACK)
+            if on_vector:
+                nc.vector.tensor_copy(dst, src[:].rearrange("p j s -> p s j"))
+            else:
+                nc.scalar.copy(dst, src[:].rearrange("p j s -> p s j"))
+            return buf
+
+        def quantize(woven, a, s0, n):
+            cw = keep.tile([P, n], U32, name="cw%d_%d" % (a, s0), align_bytes=64)
+            cs = keep.tile([P, n], U8, name="cs%d_%d" % (a, s0), align_bytes=64)
+            nc.vector.quantize_mx(out=cw[:].bitcast(FP8X4), scales=cs[:], in_=woven[:].bitcast(BF16)[:, 0:n * PACK])
+            for e in range(s0 // C, (s0 + n) // C):
+                c0 = e * C - s0
+                codes[(a, e)] = (cw[:, c0:c0 + C], cs[:, c0:c0 + C])
+
+        def product(acc, a, e, h):
+            cw, cs = codes[(a, e)]
+            nc.tensor.matmul_mx(
+                out=acc,
+                lhsT=w[e // 2][:, (e % 2) * PASSES + a, 2 * P * h:2 * P * (h + 1)].bitcast(FP4X4),
+                lhsT_scale=w_plane[:, e * PASSES + a, P * h:P * (h + 1)],
+                rhs=cw.bitcast(FP8X4),
+                rhs_scale=cs,
+                start=(a == 0),
+                stop=(a == PASSES - 1),
+            )
+
+        def finish(buf, s0, n):
+            experts = list(range(s0 // C, (s0 + n) // C))
+            bank = psum.tile([P, 4, C], F32, name="bank%d" % s0)
+            for h in range(HALVES):
+                for i, e in enumerate(experts):
+                    for a in range(PASSES):
+                        product(bank[:, 2 * h + i, :], a, e, h)
+            for h in range(HALVES):
+                r = buf[:, h * PAIR:(h + 1) * PAIR]
+                for i, e in enumerate(experts):
+                    nc.scalar.activation(r[:, i * C:(i + 1) * C], bank[:, 2 * h + i, :], ACT.Relu, bias=bias[:, h, e:e + 1])
+                nc.scalar.activation(y[h][:, s0:s0 + n], r[:, 0:n], ACT.Square)
+
+        first = [keep.tile([P, PACK, PAIR], F32, name="first%d" % g) for g in range(S // PAIR)]
+        for g in range(S // PAIR):
+            gather(first[g], 0, 0, g * PAIR, PAIR)
+        pending = []
+        for g in range(S // PAIR):
+            for j in range(1, PACK):
+                gather(first[g], 0, j, g * PAIR, PAIR)
+            for job in pending:
+                quantize(*job)
+            pending = [(weave(first[g], PAIR, stage[g % 2]), 0, g * PAIR, PAIR)]
+
+        groups = [(0, PAIR), (PAIR, PAIR), (2 * PAIR, PAIR), (3 * PAIR, C), (3 * PAIR + C, C)]
+        units = [(s0, n, a) for s0, n in groups for a in range(1, PASSES)]
+        last_banks = [psum.tile([P, 4, C], F32, name="last%d" % h) for h in range(HALVES)]
+        for u, (s0, n, a) in enumerate(units):
+            last = u == len(units) - 1
+            gated = ring.tile([P, PACK, n], F32, name="gated")
+            for j in range(PACK):
+                gather(gated, a, j, s0, n)
+            for job in pending:
+                quantize(*job)
+                if job[1] == PASSES - 1:
+                    finish(job[0], job[2], job[3])
+            if last:
+                for h in range(HALVES):
+                    for a0 in range(PASSES - 1):
+                        product(last_banks[h][:, 0, :], a0, E - 1, h)
+            pending = [(weave(gated, n, stage[2 if last else u % 2], on_vector=last), a, s0, n)]
+        quantize(*pending[0])
+        for h in range(HALVES):
+            product(last_banks[h][:, 0, :], PASSES - 1, E - 1, h)
+        s0 = S - C
+        r0 = keep.tile([P, C], F32, name="r0")
+        r1 = keep.tile([P, C], F32, name="r1")
+        nc.vector.tensor_scalar(r0[:], last_banks[0][:, 0, :], bias[:, 0, E - 1:E], 0.0, ALU.add, ALU.max)
+        nc.vector.tensor_tensor(y[0][:, s0:S], r0[:], r0[:], ALU.mult)
+        nc.scalar.activation(r1[:], last_banks[1][:, 0, :], ACT.Relu, bias=bias[:, 1, E - 1:E])
+        nc.scalar.activation(y[1][:, s0:S], r1[:], ACT.Square)
+
+        for h in range(HALVES):
+            one = keep.tile([P, T], F32, name="one%d" % h)
+            nc.vector.tensor_copy(one[:], y[h][:].indirect(pos1_t[:]))
+            both = keep.tile([P, T], F32, name="both%d" % h)
+            nc.vector.tensor_tensor(both[:], y[h][:].indirect(pos2_t[:]), one[:], ALU.add)
+            nc.sync.dma_start(out=out[h * P:(h + 1) * P, :], in_=both[:])

@@ -22,6 +22,7 @@ PACK = 4
 PASSES = K // (P * PACK)
 HALVES = N // P
 PAIR = 2 * C
+SPARE = 32
 
 
 def tile_moe_pre_lin_relu2_kernel(tc, xT, w_words, w_scales, b, gate, offs, pos1, pos2, out):
@@ -34,9 +35,8 @@ def tile_moe_pre_lin_relu2_kernel(tc, xT, w_words, w_scales, b, gate, offs, pos1
         offs_t = keep.tile([P, S // 16], U16, name="offs_t")
         pos1_t = keep.tile([P, T // 16], U16, name="pos1_t")
         pos2_t = keep.tile([P, T // 16], U16, name="pos2_t")
-        gate_a = keep.tile([P, PAIR], F32, name="gate_a")
-        gate_b = keep.tile([P, S - PAIR], F32, name="gate_b")
-        x = [[keep.tile([P, T], F32, name="x%d%d" % (a, j)) for j in range(PACK)] for a in range(PASSES)]
+        gate_t = keep.tile([P, S], F32, name="gate_t")
+        x = [[keep.tile([P, T + SPARE], F32, name="x%d%d" % (a, j)) for j in range(PACK)] for a in range(PASSES)]
         w_plane = keep.tile([P, E * PASSES, N], U8, name="w_plane", align_bytes=64)
         w = [keep.tile([P, 2 * PASSES, 2 * N], U8, name="w%d" % g, align_bytes=64) for g in range(E // 2)]
         bias = keep.tile([P, HALVES, E], F32, name="bias")
@@ -47,17 +47,21 @@ def tile_moe_pre_lin_relu2_kernel(tc, xT, w_words, w_scales, b, gate, offs, pos1
         def x_rows(a, j):
             return xT[a * P * PACK:(a + 1) * P * PACK, :].rearrange("(p j) t -> p j t", j=PACK)[:, j, :]
 
-        nc.vector.memset(w_plane[:].rearrange("p g n -> p (g n)").bitcast(I32), 0)
+        nc.gpsimd.memset(w_plane[:].rearrange("p g n -> p (g n)").bitcast(I32), 0)
         nc.vector.memset(warm[:], 0.0)
-        nc.scalar.dma_start(out=gate_a[:], in_=gate[0:P, 0:PAIR])
+        for a in range(PASSES):
+            for j in range(PACK):
+                nc.vector.memset(x[a][j][:, T:T + SPARE], 0.0)
+        nc.scalar.dma_start(out=gate_t[:, 0:PAIR], in_=gate[0:P, 0:PAIR])
         nc.sync.dma_start(offs_t[:], offs)
-        nc.sync.dma_start(out=x[0][0][:], in_=x_rows(0, 0))
-        nc.sync.dma_start(out=gate_b[:], in_=gate[0:P, PAIR:S])
+        nc.sync.dma_start(out=x[0][0][:, 0:T], in_=x_rows(0, 0))
+        nc.sync.dma_start(out=gate_t[:, PAIR:2 * PAIR], in_=gate[0:P, PAIR:2 * PAIR])
         nc.scalar.activation(warm2[:], warm[:], ACT.Relu)
         for a in range(PASSES):
             for j in range(PACK):
                 if (a, j) != (0, 0):
-                    nc.sync.dma_start(out=x[a][j][:], in_=x_rows(a, j))
+                    nc.sync.dma_start(out=x[a][j][:, 0:T], in_=x_rows(a, j))
+        nc.sync.dma_start(out=gate_t[:, 2 * PAIR:S], in_=gate[0:P, 2 * PAIR:S])
         scales = w_scales.bitcast(I32).rearrange("e a q n -> q (e a) n")
         for q in range(4):
             nc.sync.dma_start(out=w_plane[32 * q:32 * q + 4, :, :].bitcast(I32), in_=scales[4 * q:4 * q + 4])
@@ -68,30 +72,36 @@ def tile_moe_pre_lin_relu2_kernel(tc, xT, w_words, w_scales, b, gate, offs, pos1
         nc.sync.dma_start(pos1_t[:], pos1)
         nc.sync.dma_start(pos2_t[:], pos2)
 
-        def gate_cols(s0, n):
-            return gate_a[:, s0:s0 + n] if s0 < PAIR else gate_b[:, s0 - PAIR:s0 - PAIR + n]
+        codes = {}
 
         def gather(dst, a, j, s0, n):
             window = x[a][j][:].indirect(offs_t[:, s0 // 16:(s0 + n) // 16])
-            nc.vector.tensor_tensor(dst[:, j, :], window, gate_cols(s0, n), ALU.mult)
+            nc.vector.tensor_tensor(dst, window, gate_t[:, s0:s0 + n], ALU.mult)
 
-        codes = {}
+        def gather_unit(a, s0, n):
+            gated = ring.tile([P, PACK, n], F32, name="gated")
+            for j in range(PACK):
+                if (a, j, s0) == (0, 0, 0):
+                    gather(gated[:, j, 0:PAIR], a, j, 0, PAIR)
+                    gather(gated[:, j, PAIR:n], a, j, PAIR, n - PAIR)
+                else:
+                    gather(gated[:, j, :], a, j, s0, n)
+            return gated
 
-        stage = [keep.tile([P, 2 * PAIR], F32, name="stage%d" % i, align_bytes=64) for i in range(3)]
+        def stage(a, s0, n):
+            return keep.tile([P, 2 * n], F32, name="stage%d_%d" % (a, s0), align_bytes=64)
 
-        def weave(src, n, buf, on_vector=False):
-            woven = buf[:].bitcast(BF16)[:, 0:n * PACK]
-            dst = woven.rearrange("p (s j) -> p s j", j=PACK)
+        def weave(buf, src, on_vector=False):
+            dst = buf[:].bitcast(BF16).rearrange("p (s j) -> p s j", j=PACK)
             if on_vector:
-                nc.vector.tensor_copy(dst, src[:].rearrange("p j s -> p s j"))
+                nc.vector.tensor_copy(dst, src.rearrange("p j s -> p s j"))
             else:
-                nc.scalar.copy(dst, src[:].rearrange("p j s -> p s j"))
-            return buf
+                nc.scalar.copy(dst, src.rearrange("p j s -> p s j"))
 
-        def quantize(woven, a, s0, n):
+        def quantize(buf, a, s0, n):
             cw = keep.tile([P, n], U32, name="cw%d_%d" % (a, s0), align_bytes=64)
             cs = keep.tile([P, n], U8, name="cs%d_%d" % (a, s0), align_bytes=64)
-            nc.vector.quantize_mx(out=cw[:].bitcast(FP8X4), scales=cs[:], in_=woven[:].bitcast(BF16)[:, 0:n * PACK])
+            nc.vector.quantize_mx(out=cw[:].bitcast(FP8X4), scales=cs[:], in_=buf[:].bitcast(BF16))
             for e in range(s0 // C, (s0 + n) // C):
                 c0 = e * C - s0
                 codes[(a, e)] = (cw[:, c0:c0 + C], cs[:, c0:c0 + C])
@@ -108,56 +118,87 @@ def tile_moe_pre_lin_relu2_kernel(tc, xT, w_words, w_scales, b, gate, offs, pos1
                 stop=(a == PASSES - 1),
             )
 
-        def finish(buf, s0, n):
-            experts = list(range(s0 // C, (s0 + n) // C))
-            bank = psum.tile([P, 4, C], F32, name="bank%d" % s0)
-            for h in range(HALVES):
-                for i, e in enumerate(experts):
-                    for a in range(PASSES):
-                        product(bank[:, 2 * h + i, :], a, e, h)
-            for h in range(HALVES):
-                r = buf[:, h * PAIR:(h + 1) * PAIR]
-                for i, e in enumerate(experts):
-                    nc.scalar.activation(r[:, i * C:(i + 1) * C], bank[:, 2 * h + i, :], ACT.Relu, bias=bias[:, h, e:e + 1])
-                nc.scalar.activation(y[h][:, s0:s0 + n], r[:, 0:n], ACT.Square)
+        banks = [psum.tile([P, 4, C], F32, name="bank%d" % i) for i in range(8)]
 
-        first = [keep.tile([P, PACK, PAIR], F32, name="first%d" % g) for g in range(S // PAIR)]
-        for g in range(S // PAIR):
-            gather(first[g], 0, 0, g * PAIR, PAIR)
-        pending = []
-        for g in range(S // PAIR):
-            for j in range(1, PACK):
-                gather(first[g], 0, j, g * PAIR, PAIR)
-            for job in pending:
-                quantize(*job)
-            pending = [(weave(first[g], PAIR, stage[g % 2]), 0, g * PAIR, PAIR)]
+        def acc(e, h):
+            if e < 4:
+                return banks[e // 2][:, 2 * h + e % 2, :]
+            if e < 6:
+                return banks[(2 + 2 * h + e % 2) % 4][:, 0, :]
+            return banks[4 + 2 * (e - 6) + h][:, 0, :]
 
-        groups = [(0, PAIR), (PAIR, PAIR), (2 * PAIR, PAIR), (3 * PAIR, C), (3 * PAIR + C, C)]
-        units = [(s0, n, a) for s0, n in groups for a in range(1, PASSES)]
-        last_banks = [psum.tile([P, 4, C], F32, name="last%d" % h) for h in range(HALVES)]
-        for u, (s0, n, a) in enumerate(units):
-            last = u == len(units) - 1
-            gated = ring.tile([P, PACK, n], F32, name="gated")
-            for j in range(PACK):
-                gather(gated, a, j, s0, n)
-            for job in pending:
-                quantize(*job)
-                if job[1] == PASSES - 1:
-                    finish(job[0], job[2], job[3])
-            if last:
-                for h in range(HALVES):
-                    for a0 in range(PASSES - 1):
-                        product(last_banks[h][:, 0, :], a0, E - 1, h)
-            pending = [(weave(gated, n, stage[2 if last else u % 2], on_vector=last), a, s0, n)]
-        quantize(*pending[0])
-        for h in range(HALVES):
-            product(last_banks[h][:, 0, :], PASSES - 1, E - 1, h)
+        def products(experts, passes):
+            for h in range(HALVES):
+                for e in experts:
+                    for a in passes:
+                        product(acc(e, h), a, e, h)
+
+        def finish(buf, experts):
+            n = len(experts) * C
+            s0 = experts[0] * C
+            for h in range(HALVES):
+                r = buf[:, h * n:(h + 1) * n]
+                for i, e in enumerate(experts):
+                    nc.scalar.activation(r[:, i * C:(i + 1) * C], acc(e, h), ACT.Relu, bias=bias[:, h, e:e + 1])
+                nc.scalar.activation(y[h][:, s0:s0 + n], r, ACT.Square)
+
+        A, B, CC, DD = 0, 4 * C, 6 * C, 7 * C
+        a0, a1 = stage(0, A, 2 * PAIR), stage(1, A, 2 * PAIR)
+        a2a, a2b = stage(2, A, PAIR), stage(2, A + PAIR, PAIR)
+        b0, b1, b2 = stage(0, B, PAIR), stage(1, B, PAIR), stage(2, B, PAIR)
+        c0, c1 = stage(0, CC, PAIR), stage(1, CC, PAIR)
+        c2, d2 = stage(2, CC, C), stage(2, DD, C)
+        rc = keep.tile([P, 2 * C], F32, name="rc")
+
+        g = gather_unit(0, A, 2 * PAIR)
+        weave(a0, g[:])
+        g = gather_unit(1, A, 2 * PAIR)
+        quantize(a0, 0, A, 2 * PAIR)
+        weave(a1, g[:])
+        g = gather_unit(2, A, 2 * PAIR)
+        quantize(a1, 1, A, 2 * PAIR)
+        weave(a2a, g[:, :, 0:PAIR])
+        weave(a2b, g[:, :, PAIR:2 * PAIR])
+        g = gather_unit(0, B, PAIR)
+        quantize(a2a, 2, A, PAIR)
+        products([0, 1], range(PASSES))
+        quantize(a2b, 2, A + PAIR, PAIR)
+        products([2, 3], range(PASSES))
+        weave(b0, g[:])
+        g = gather_unit(1, B, PAIR)
+        quantize(b0, 0, B, PAIR)
+        finish(b1, [0, 1])
+        weave(b1, g[:])
+        g = gather_unit(2, B, PAIR)
+        quantize(b1, 1, B, PAIR)
+        finish(b2, [2, 3])
+        weave(b2, g[:])
+        products([4, 5], range(PASSES - 1))
+        g = gather_unit(0, CC, PAIR)
+        quantize(b2, 2, B, PAIR)
+        products([4, 5], [PASSES - 1])
+        weave(c0, g[:])
+        g = gather_unit(1, CC, PAIR)
+        quantize(c0, 0, CC, PAIR)
+        finish(c1, [4, 5])
+        weave(c1, g[:])
+        g = gather_unit(2, CC, C)
+        quantize(c1, 1, CC, PAIR)
+        products([6, 7], range(PASSES - 1))
+        weave(c2, g[:])
+        g = gather_unit(2, DD, C)
+        quantize(c2, 2, CC, C)
+        products([6], [PASSES - 1])
+        finish(rc, [6])
+        weave(d2, g[:], on_vector=True)
+        quantize(d2, 2, DD, C)
+        products([7], [PASSES - 1])
         s0 = S - C
         r0 = keep.tile([P, C], F32, name="r0")
         r1 = keep.tile([P, C], F32, name="r1")
-        nc.vector.tensor_scalar(r0[:], last_banks[0][:, 0, :], bias[:, 0, E - 1:E], 0.0, ALU.add, ALU.max)
+        nc.vector.tensor_scalar(r0[:], acc(E - 1, 0), bias[:, 0, E - 1:E], 0.0, ALU.add, ALU.max)
         nc.vector.tensor_tensor(y[0][:, s0:S], r0[:], r0[:], ALU.mult)
-        nc.scalar.activation(r1[:], last_banks[1][:, 0, :], ACT.Relu, bias=bias[:, 1, E - 1:E])
+        nc.scalar.activation(r1[:], acc(E - 1, 1), ACT.Relu, bias=bias[:, 1, E - 1:E])
         nc.scalar.activation(y[1][:, s0:S], r1[:], ACT.Square)
 
         for h in range(HALVES):

@@ -22,7 +22,7 @@ PACK = 4
 PASSES = K // (P * PACK)
 HALVES = N // P
 PAIR = 2 * C
-SPARE = 32
+SPARE = 160
 
 
 def tile_moe_pre_lin_relu2_kernel(tc, xT, w_words, w_scales, b, gate, offs, pos1, pos2, out):
@@ -49,19 +49,16 @@ def tile_moe_pre_lin_relu2_kernel(tc, xT, w_words, w_scales, b, gate, offs, pos1
 
         nc.gpsimd.memset(w_plane[:].rearrange("p g n -> p (g n)").bitcast(I32), 0)
         nc.vector.memset(warm[:], 0.0)
-        for a in range(PASSES):
-            for j in range(PACK):
-                nc.vector.memset(x[a][j][:, T:T + SPARE], 0.0)
         nc.scalar.dma_start(out=gate_t[:, 0:PAIR], in_=gate[0:P, 0:PAIR])
-        nc.sync.dma_start(offs_t[:], offs)
         nc.sync.dma_start(out=x[0][0][:, 0:T], in_=x_rows(0, 0))
-        nc.sync.dma_start(out=gate_t[:, PAIR:2 * PAIR], in_=gate[0:P, PAIR:2 * PAIR])
+        nc.sync.dma_start(offs_t[:], offs)
+        nc.sync.dma_start(out=gate_t[:, PAIR:5 * C], in_=gate[0:P, PAIR:5 * C])
         nc.scalar.activation(warm2[:], warm[:], ACT.Relu)
         for a in range(PASSES):
             for j in range(PACK):
                 if (a, j) != (0, 0):
                     nc.sync.dma_start(out=x[a][j][:, 0:T], in_=x_rows(a, j))
-        nc.sync.dma_start(out=gate_t[:, 2 * PAIR:S], in_=gate[0:P, 2 * PAIR:S])
+        nc.sync.dma_start(out=gate_t[:, 5 * C:S], in_=gate[0:P, 5 * C:S])
         scales = w_scales.bitcast(I32).rearrange("e a q n -> q (e a) n")
         for q in range(4):
             nc.sync.dma_start(out=w_plane[32 * q:32 * q + 4, :, :].bitcast(I32), in_=scales[4 * q:4 * q + 4])
@@ -92,16 +89,17 @@ def tile_moe_pre_lin_relu2_kernel(tc, xT, w_words, w_scales, b, gate, offs, pos1
             return keep.tile([P, 2 * n], F32, name="stage%d_%d" % (a, s0), align_bytes=64)
 
         def weave(buf, src, on_vector=False):
-            dst = buf[:].bitcast(BF16).rearrange("p (s j) -> p s j", j=PACK)
+            dst = buf[:].bitcast(BF16).rearrange("p (c i j) -> p c j i", i=4, j=PACK)
+            walk = src.rearrange("p j (c i) -> p c j i", i=4)
             if on_vector:
-                nc.vector.tensor_copy(dst, src.rearrange("p j s -> p s j"))
+                nc.vector.tensor_copy(dst, walk)
             else:
-                nc.scalar.copy(dst, src.rearrange("p j s -> p s j"))
+                nc.scalar.copy(dst, walk)
 
         def quantize(buf, a, s0, n):
             cw = keep.tile([P, n], U32, name="cw%d_%d" % (a, s0), align_bytes=64)
             cs = keep.tile([P, n], U8, name="cs%d_%d" % (a, s0), align_bytes=64)
-            nc.vector.quantize_mx(out=cw[:].bitcast(FP8X4), scales=cs[:], in_=buf[:].bitcast(BF16))
+            nc.vector.quantize_mx(out=cw[:].bitcast(FP8X4), scales=cs[:], in_=buf.bitcast(BF16))
             for e in range(s0 // C, (s0 + n) // C):
                 c0 = e * C - s0
                 codes[(a, e)] = (cw[:, c0:c0 + C], cs[:, c0:c0 + C])
@@ -123,9 +121,11 @@ def tile_moe_pre_lin_relu2_kernel(tc, xT, w_words, w_scales, b, gate, offs, pos1
         def acc(e, h):
             if e < 4:
                 return banks[e // 2][:, 2 * h + e % 2, :]
-            if e < 6:
-                return banks[(2 + 2 * h + e % 2) % 4][:, 0, :]
-            return banks[4 + 2 * (e - 6) + h][:, 0, :]
+            if e == 4:
+                return banks[2][:, h, :]
+            if e < 7:
+                return banks[(3 + 2 * h + e - 5) % 6][:, 0, :]
+            return banks[6 + h][:, 0, :]
 
         def products(experts, passes):
             for h in range(HALVES):
@@ -142,56 +142,51 @@ def tile_moe_pre_lin_relu2_kernel(tc, xT, w_words, w_scales, b, gate, offs, pos1
                     nc.scalar.activation(r[:, i * C:(i + 1) * C], acc(e, h), ACT.Relu, bias=bias[:, h, e:e + 1])
                 nc.scalar.activation(y[h][:, s0:s0 + n], r, ACT.Square)
 
-        A, B, CC, DD = 0, 4 * C, 6 * C, 7 * C
-        a0, a1 = stage(0, A, 2 * PAIR), stage(1, A, 2 * PAIR)
-        a2a, a2b = stage(2, A, PAIR), stage(2, A + PAIR, PAIR)
-        b0, b1, b2 = stage(0, B, PAIR), stage(1, B, PAIR), stage(2, B, PAIR)
-        c0, c1 = stage(0, CC, PAIR), stage(1, CC, PAIR)
-        c2, d2 = stage(2, CC, C), stage(2, DD, C)
-        rc = keep.tile([P, 2 * C], F32, name="rc")
+        NA, NR = 5 * C, 3 * C
+        a0, a1 = stage(0, 0, NA), stage(1, 0, NA)
+        a2a, a2b, a2c = stage(2, 0, PAIR), stage(2, PAIR, PAIR), stage(2, 2 * PAIR, C)
+        rest0, rest1 = stage(0, NA, NR), stage(1, NA, NR)
+        b2, d2 = stage(2, NA, PAIR), stage(2, NA + PAIR, C)
+        rb = keep.tile([P, 2 * PAIR], F32, name="rb")
 
-        g = gather_unit(0, A, 2 * PAIR)
+        def quantize_two(buf, a, s0, n1, n2):
+            quantize(buf[:, 0:2 * n1], a, s0, n1)
+            quantize(buf[:, 2 * n1:2 * (n1 + n2)], a, s0 + n1, n2)
+
+        g = gather_unit(0, 0, NA)
         weave(a0, g[:])
-        g = gather_unit(1, A, 2 * PAIR)
-        quantize(a0, 0, A, 2 * PAIR)
+        g = gather_unit(1, 0, NA)
+        quantize_two(a0, 0, 0, 2 * PAIR, C)
         weave(a1, g[:])
-        g = gather_unit(2, A, 2 * PAIR)
-        quantize(a1, 1, A, 2 * PAIR)
+        g = gather_unit(2, 0, NA)
+        quantize_two(a1, 1, 0, 2 * PAIR, C)
         weave(a2a, g[:, :, 0:PAIR])
         weave(a2b, g[:, :, PAIR:2 * PAIR])
-        g = gather_unit(0, B, PAIR)
-        quantize(a2a, 2, A, PAIR)
+        weave(a2c, g[:, :, 2 * PAIR:NA])
+        quantize(a2a[:], 2, 0, PAIR)
         products([0, 1], range(PASSES))
-        quantize(a2b, 2, A + PAIR, PAIR)
+        g = gather_unit(0, NA, NR)
+        quantize(a2b[:], 2, PAIR, PAIR)
         products([2, 3], range(PASSES))
-        weave(b0, g[:])
-        g = gather_unit(1, B, PAIR)
-        quantize(b0, 0, B, PAIR)
-        finish(b1, [0, 1])
-        weave(b1, g[:])
-        g = gather_unit(2, B, PAIR)
-        quantize(b1, 1, B, PAIR)
+        quantize(a2c[:], 2, 2 * PAIR, C)
+        products([4], range(PASSES))
+        weave(rest0, g[:])
+        g = gather_unit(1, NA, NR)
+        quantize_two(rest0, 0, NA, PAIR, C)
+        finish(rest1, [0, 1])
         finish(b2, [2, 3])
+        weave(rest1, g[:])
+        g = gather_unit(2, NA, PAIR)
+        quantize_two(rest1, 1, NA, PAIR, C)
+        products([5, 6, 7], range(PASSES - 1))
         weave(b2, g[:])
-        products([4, 5], range(PASSES - 1))
-        g = gather_unit(0, CC, PAIR)
-        quantize(b2, 2, B, PAIR)
-        products([4, 5], [PASSES - 1])
-        weave(c0, g[:])
-        g = gather_unit(1, CC, PAIR)
-        quantize(c0, 0, CC, PAIR)
-        finish(c1, [4, 5])
-        weave(c1, g[:])
-        g = gather_unit(2, CC, C)
-        quantize(c1, 1, CC, PAIR)
-        products([6, 7], range(PASSES - 1))
-        weave(c2, g[:])
-        g = gather_unit(2, DD, C)
-        quantize(c2, 2, CC, C)
-        products([6], [PASSES - 1])
-        finish(rc, [6])
+        finish(g[:, 0, :], [4])
+        g = gather_unit(2, NA + PAIR, C)
+        quantize(b2[:], 2, NA, PAIR)
+        products([5, 6], [PASSES - 1])
+        finish(rb, [5, 6])
         weave(d2, g[:], on_vector=True)
-        quantize(d2, 2, DD, C)
+        quantize(d2[:], 2, NA + PAIR, C)
         products([7], [PASSES - 1])
         s0 = S - C
         r0 = keep.tile([P, C], F32, name="r0")
@@ -201,9 +196,10 @@ def tile_moe_pre_lin_relu2_kernel(tc, xT, w_words, w_scales, b, gate, offs, pos1
         nc.scalar.activation(r1[:], acc(E - 1, 1), ACT.Relu, bias=bias[:, 1, E - 1:E])
         nc.scalar.activation(y[1][:, s0:S], r1[:], ACT.Square)
 
+        one = [keep.tile([P, T], F32, name="one%d" % h) for h in range(HALVES)]
+        both = [keep.tile([P, T], F32, name="both%d" % h) for h in range(HALVES)]
         for h in range(HALVES):
-            one = keep.tile([P, T], F32, name="one%d" % h)
-            nc.vector.tensor_copy(one[:], y[h][:].indirect(pos1_t[:]))
-            both = keep.tile([P, T], F32, name="both%d" % h)
-            nc.vector.tensor_tensor(both[:], y[h][:].indirect(pos2_t[:]), one[:], ALU.add)
-            nc.sync.dma_start(out=out[h * P:(h + 1) * P, :], in_=both[:])
+            nc.vector.tensor_copy(one[h][:], y[h][:].indirect(pos1_t[:]))
+        for h, t0, t1 in ((0, 0, T), (1, 0, T - C), (1, T - C, T)):
+            nc.vector.tensor_tensor(both[h][:, t0:t1], y[h][:].indirect(pos2_t[:, t0 // 16:t1 // 16]), one[h][:, t0:t1], ALU.add)
+            nc.sync.dma_start(out=out[h * P:(h + 1) * P, t0:t1], in_=both[h][:, t0:t1])

@@ -5,6 +5,7 @@ import concourse.mybir as mybir
 K, T, E, C, N = 1536, 512, 8, 128, 256
 S = E * C
 FLOPS = 2 * K * N * S
+BYTES = 4 * K * T + E * K * N // 2 + E * K * N // 32 + 4 * N * E + 4 * S + 2 * 128 * (S + 2 * T) // 16 + 4 * N * T
 
 F32 = mybir.dt.float32
 BF16 = mybir.dt.bfloat16
@@ -20,9 +21,13 @@ ACT = mybir.ActivationFunctionType
 P = 128
 PACK = 4
 PASSES = K // (P * PACK)
+LAST = PASSES - 1
 HALVES = N // P
+STRIPE = 16
 PAIR = 2 * C
-SPARE = 160
+FRONT = 5 * C
+REST = S - FRONT
+WINDOW = FRONT + 32
 
 
 def tile_moe_pre_lin_relu2_kernel(tc, xT, w_words, w_scales, b, gate, offs, pos1, pos2, out):
@@ -32,174 +37,167 @@ def tile_moe_pre_lin_relu2_kernel(tc, xT, w_words, w_scales, b, gate, offs, pos1
         ring = ctx.enter_context(tc.tile_pool(name="ring", bufs=2))
         psum = ctx.enter_context(tc.psum_pool(name="psum", bufs=1))
 
-        offs_t = keep.tile([P, S // 16], U16, name="offs_t")
-        pos1_t = keep.tile([P, T // 16], U16, name="pos1_t")
-        pos2_t = keep.tile([P, T // 16], U16, name="pos2_t")
+        offs_t = keep.tile([P, S // STRIPE], U16, name="offs_t")
+        pos1_t = keep.tile([P, T // STRIPE], U16, name="pos1_t")
+        pos2_t = keep.tile([P, T // STRIPE], U16, name="pos2_t")
         gate_t = keep.tile([P, S], F32, name="gate_t")
-        x = [[keep.tile([P, T + SPARE], F32, name="x%d%d" % (a, j)) for j in range(PACK)] for a in range(PASSES)]
-        w_plane = keep.tile([P, E * PASSES, N], U8, name="w_plane", align_bytes=64)
-        w = [keep.tile([P, 2 * PASSES, 2 * N], U8, name="w%d" % g, align_bytes=64) for g in range(E // 2)]
+        planes = [[keep.tile([P, WINDOW], F32, name="plane%d%d" % (a, j)) for j in range(PACK)] for a in range(PASSES)]
+        w_scale_t = keep.tile([P, E * PASSES, N], U8, name="w_scale_t", align_bytes=64)
+        w_word_t = [keep.tile([P, 2 * PASSES, 2 * N], U8, name="w_word_t%d" % g, align_bytes=64) for g in range(E // 2)]
         bias = keep.tile([P, HALVES, E], F32, name="bias")
         y = [keep.tile([P, S], F32, name="y%d" % h) for h in range(HALVES)]
-        warm = keep.tile([P, 8], F32, name="warm")
-        warm2 = keep.tile([P, 8], F32, name="warm2")
 
-        def x_rows(a, j):
-            return xT[a * P * PACK:(a + 1) * P * PACK, :].rearrange("(p j) t -> p j t", j=PACK)[:, j, :]
+        def load_plane(a, j):
+            rows = xT[a * P * PACK:(a + 1) * P * PACK, :].rearrange("(p j) t -> p j t", j=PACK)
+            nc.sync.dma_start(out=planes[a][j][:, 0:T], in_=rows[:, j, :])
 
-        nc.gpsimd.memset(w_plane[:].rearrange("p g n -> p (g n)").bitcast(I32), 0)
-        nc.vector.memset(warm[:], 0.0)
-        nc.scalar.dma_start(out=gate_t[:, 0:PAIR], in_=gate[0:P, 0:PAIR])
-        nc.sync.dma_start(out=x[0][0][:, 0:T], in_=x_rows(0, 0))
+        def load_gate(queue, s0, s1):
+            queue.dma_start(out=gate_t[:, s0:s1], in_=gate[0:P, s0:s1])
+
+        nc.gpsimd.memset(w_scale_t[:].rearrange("p g n -> p (g n)").bitcast(I32), 0)
+
+        load_gate(nc.scalar, 0, PAIR)
+        load_plane(0, 0)
         nc.sync.dma_start(offs_t[:], offs)
-        nc.sync.dma_start(out=gate_t[:, PAIR:5 * C], in_=gate[0:P, PAIR:5 * C])
-        nc.scalar.activation(warm2[:], warm[:], ACT.Relu)
+        load_gate(nc.sync, PAIR, FRONT)
         for a in range(PASSES):
             for j in range(PACK):
                 if (a, j) != (0, 0):
-                    nc.sync.dma_start(out=x[a][j][:, 0:T], in_=x_rows(a, j))
-        nc.sync.dma_start(out=gate_t[:, 5 * C:S], in_=gate[0:P, 5 * C:S])
-        scales = w_scales.bitcast(I32).rearrange("e a q n -> q (e a) n")
-        for q in range(4):
-            nc.sync.dma_start(out=w_plane[32 * q:32 * q + 4, :, :].bitcast(I32), in_=scales[4 * q:4 * q + 4])
-        words = w_words.bitcast(I32).rearrange("e a p n -> p (e a) n")
+                    load_plane(a, j)
+        load_gate(nc.sync, FRONT, S)
+        scale_rows = w_scales.bitcast(I32).rearrange("e a q n -> q (e a) n")
+        for quad in range(4):
+            nc.sync.dma_start(out=w_scale_t[32 * quad:32 * quad + 4, :, :].bitcast(I32), in_=scale_rows[4 * quad:4 * quad + 4])
+        word_rows = w_words.bitcast(I32).rearrange("e a p n -> p (e a) n")
         for g in range(E // 2):
-            nc.sync.dma_start(out=w[g][:].bitcast(I32), in_=words[:, 2 * PASSES * g:2 * PASSES * (g + 1), :])
+            nc.sync.dma_start(out=w_word_t[g][:].bitcast(I32), in_=word_rows[:, 2 * PASSES * g:2 * PASSES * (g + 1), :])
         nc.sync.dma_start(out=bias[:], in_=b.rearrange("(h p) e -> p h e", p=P))
         nc.sync.dma_start(pos1_t[:], pos1)
         nc.sync.dma_start(pos2_t[:], pos2)
 
-        codes = {}
-
-        def gather(dst, a, j, s0, n):
-            window = x[a][j][:].indirect(offs_t[:, s0 // 16:(s0 + n) // 16])
-            nc.vector.tensor_tensor(dst, window, gate_t[:, s0:s0 + n], ALU.mult)
+        def gather(dst, a, j, s0, s1):
+            window = planes[a][j][:].indirect(offs_t[:, s0 // STRIPE:s1 // STRIPE])
+            nc.vector.tensor_tensor(dst, window, gate_t[:, s0:s1], ALU.mult)
 
         def gather_unit(a, s0, n):
             gated = ring.tile([P, PACK, n], F32, name="gated")
             for j in range(PACK):
                 if (a, j, s0) == (0, 0, 0):
                     gather(gated[:, j, 0:PAIR], a, j, 0, PAIR)
-                    gather(gated[:, j, PAIR:n], a, j, PAIR, n - PAIR)
+                    gather(gated[:, j, PAIR:n], a, j, PAIR, n)
                 else:
-                    gather(gated[:, j, :], a, j, s0, n)
+                    gather(gated[:, j, :], a, j, s0, s0 + n)
             return gated
 
-        def stage(a, s0, n):
-            return keep.tile([P, 2 * n], F32, name="stage%d_%d" % (a, s0), align_bytes=64)
+        def woven_tile(a, s0, n):
+            return keep.tile([P, 2 * n], F32, name="woven%d_%d" % (a, s0), align_bytes=64)
 
-        def weave(buf, src, on_vector=False):
-            dst = buf[:].bitcast(BF16).rearrange("p (c i j) -> p c j i", i=4, j=PACK)
-            walk = src.rearrange("p j (c i) -> p c j i", i=4)
-            if on_vector:
-                nc.vector.tensor_copy(dst, walk)
-            else:
-                nc.scalar.copy(dst, walk)
+        def weave_views(woven, gated):
+            dst = woven[:].bitcast(BF16).rearrange("p (c i j) -> p c j i", i=4, j=PACK)
+            return dst, gated.rearrange("p j (c i) -> p c j i", i=4)
 
-        def quantize(buf, a, s0, n):
-            cw = keep.tile([P, n], U32, name="cw%d_%d" % (a, s0), align_bytes=64)
-            cs = keep.tile([P, n], U8, name="cs%d_%d" % (a, s0), align_bytes=64)
-            nc.vector.quantize_mx(out=cw[:].bitcast(FP8X4), scales=cs[:], in_=buf.bitcast(BF16))
+        def weave(woven, gated):
+            nc.scalar.activation(*weave_views(woven, gated), ACT.Copy)
+
+        codes = {}
+
+        def quantize(woven, a, s0, n):
+            words = keep.tile([P, n], U32, name="x_words%d_%d" % (a, s0), align_bytes=64)
+            scales = keep.tile([P, n], U8, name="x_scales%d_%d" % (a, s0), align_bytes=64)
+            nc.vector.quantize_mx(out=words[:].bitcast(FP8X4), scales=scales[:], in_=woven.bitcast(BF16))
             for e in range(s0 // C, (s0 + n) // C):
                 c0 = e * C - s0
-                codes[(a, e)] = (cw[:, c0:c0 + C], cs[:, c0:c0 + C])
+                codes[(a, e)] = (words[:, c0:c0 + C], scales[:, c0:c0 + C])
 
-        def product(acc, a, e, h):
-            cw, cs = codes[(a, e)]
-            nc.tensor.matmul_mx(
-                out=acc,
-                lhsT=w[e // 2][:, (e % 2) * PASSES + a, 2 * P * h:2 * P * (h + 1)].bitcast(FP4X4),
-                lhsT_scale=w_plane[:, e * PASSES + a, P * h:P * (h + 1)],
-                rhs=cw.bitcast(FP8X4),
-                rhs_scale=cs,
-                start=(a == 0),
-                stop=(a == PASSES - 1),
-            )
+        def quantize_odd(woven, a, s0, n):
+            quantize(woven[:, 0:2 * (n - C)], a, s0, n - C)
+            quantize(woven[:, 2 * (n - C):2 * n], a, s0 + n - C, C)
 
         banks = [psum.tile([P, 4, C], F32, name="bank%d" % i) for i in range(8)]
+        rest_bank = {(5, 0): 3, (6, 0): 4, (5, 1): 5, (6, 1): 0, (7, 0): 6, (7, 1): 7}
 
         def acc(e, h):
-            if e < 4:
-                return banks[e // 2][:, 2 * h + e % 2, :]
-            if e == 4:
-                return banks[2][:, h, :]
-            if e < 7:
-                return banks[(3 + 2 * h + e - 5) % 6][:, 0, :]
-            return banks[6 + h][:, 0, :]
+            if (e, h) in rest_bank:
+                return banks[rest_bank[(e, h)]][:, 0, :]
+            return banks[e // 2][:, 2 * h + e % 2, :]
 
         def products(experts, passes):
             for h in range(HALVES):
                 for e in experts:
                     for a in passes:
-                        product(acc(e, h), a, e, h)
+                        words, scales = codes[(a, e)]
+                        nc.tensor.matmul_mx(
+                            out=acc(e, h),
+                            lhsT=w_word_t[e // 2][:, (e % 2) * PASSES + a, 2 * P * h:2 * P * (h + 1)].bitcast(FP4X4),
+                            lhsT_scale=w_scale_t[:, e * PASSES + a, P * h:P * (h + 1)],
+                            rhs=words.bitcast(FP8X4),
+                            rhs_scale=scales,
+                            start=(a == 0),
+                            stop=(a == LAST),
+                        )
+
+        def relu2(buf, experts, h):
+            for i, e in enumerate(experts):
+                nc.scalar.activation(buf[:, i * C:(i + 1) * C], acc(e, h), ACT.Relu, bias=bias[:, h, e:e + 1])
+            nc.scalar.activation(y[h][:, experts[0] * C:(experts[-1] + 1) * C], buf, ACT.Square)
 
         def finish(buf, experts):
             n = len(experts) * C
-            s0 = experts[0] * C
             for h in range(HALVES):
-                r = buf[:, h * n:(h + 1) * n]
-                for i, e in enumerate(experts):
-                    nc.scalar.activation(r[:, i * C:(i + 1) * C], acc(e, h), ACT.Relu, bias=bias[:, h, e:e + 1])
-                nc.scalar.activation(y[h][:, s0:s0 + n], r, ACT.Square)
+                relu2(buf[:, h * n:(h + 1) * n], experts, h)
 
-        NA, NR = 5 * C, 3 * C
-        a0, a1 = stage(0, 0, NA), stage(1, 0, NA)
-        a2a, a2b, a2c = stage(2, 0, PAIR), stage(2, PAIR, PAIR), stage(2, 2 * PAIR, C)
-        rest0, rest1 = stage(0, NA, NR), stage(1, NA, NR)
-        b2, d2 = stage(2, NA, PAIR), stage(2, NA + PAIR, C)
-        rb = keep.tile([P, 2 * PAIR], F32, name="rb")
+        front0, front1 = woven_tile(0, 0, FRONT), woven_tile(1, 0, FRONT)
+        last01, last23, last4 = woven_tile(LAST, 0, PAIR), woven_tile(LAST, PAIR, PAIR), woven_tile(LAST, 2 * PAIR, C)
+        rest0, rest1 = woven_tile(0, FRONT, REST), woven_tile(1, FRONT, REST)
+        last56, last7 = woven_tile(LAST, FRONT, PAIR), woven_tile(LAST, S - C, C)
 
-        def quantize_two(buf, a, s0, n1, n2):
-            quantize(buf[:, 0:2 * n1], a, s0, n1)
-            quantize(buf[:, 2 * n1:2 * (n1 + n2)], a, s0 + n1, n2)
-
-        g = gather_unit(0, 0, NA)
-        weave(a0, g[:])
-        g = gather_unit(1, 0, NA)
-        quantize_two(a0, 0, 0, 2 * PAIR, C)
-        weave(a1, g[:])
-        g = gather_unit(2, 0, NA)
-        quantize_two(a1, 1, 0, 2 * PAIR, C)
-        weave(a2a, g[:, :, 0:PAIR])
-        weave(a2b, g[:, :, PAIR:2 * PAIR])
-        weave(a2c, g[:, :, 2 * PAIR:NA])
-        quantize(a2a[:], 2, 0, PAIR)
+        gated = gather_unit(0, 0, FRONT)
+        weave(front0, gated[:])
+        gated = gather_unit(1, 0, FRONT)
+        quantize_odd(front0, 0, 0, FRONT)
+        weave(front1, gated[:])
+        gated = gather_unit(LAST, 0, FRONT)
+        quantize_odd(front1, 1, 0, FRONT)
+        weave(last01, gated[:, :, 0:PAIR])
+        weave(last23, gated[:, :, PAIR:2 * PAIR])
+        weave(last4, gated[:, :, 2 * PAIR:FRONT])
+        quantize(last01[:], LAST, 0, PAIR)
         products([0, 1], range(PASSES))
-        g = gather_unit(0, NA, NR)
-        quantize(a2b[:], 2, PAIR, PAIR)
-        products([2, 3], range(PASSES))
-        quantize(a2c[:], 2, 2 * PAIR, C)
-        products([4], range(PASSES))
-        weave(rest0, g[:])
-        g = gather_unit(1, NA, NR)
-        quantize_two(rest0, 0, NA, PAIR, C)
-        finish(rest1, [0, 1])
-        finish(b2, [2, 3])
-        weave(rest1, g[:])
-        g = gather_unit(2, NA, PAIR)
-        quantize_two(rest1, 1, NA, PAIR, C)
-        products([5, 6, 7], range(PASSES - 1))
-        weave(b2, g[:])
-        finish(g[:, 0, :], [4])
-        g = gather_unit(2, NA + PAIR, C)
-        quantize(b2[:], 2, NA, PAIR)
-        products([5, 6], [PASSES - 1])
-        finish(rb, [5, 6])
-        weave(d2, g[:], on_vector=True)
-        quantize(d2[:], 2, NA + PAIR, C)
-        products([7], [PASSES - 1])
-        s0 = S - C
-        r0 = keep.tile([P, C], F32, name="r0")
-        r1 = keep.tile([P, C], F32, name="r1")
-        nc.vector.tensor_scalar(r0[:], acc(E - 1, 0), bias[:, 0, E - 1:E], 0.0, ALU.add, ALU.max)
-        nc.vector.tensor_tensor(y[0][:, s0:S], r0[:], r0[:], ALU.mult)
-        nc.scalar.activation(r1[:], acc(E - 1, 1), ACT.Relu, bias=bias[:, 1, E - 1:E])
-        nc.scalar.activation(y[1][:, s0:S], r1[:], ACT.Square)
 
-        one = [keep.tile([P, T], F32, name="one%d" % h) for h in range(HALVES)]
+        gated = gather_unit(0, FRONT, REST)
+        quantize(last23[:], LAST, PAIR, PAIR)
+        products([2, 3], range(PASSES))
+        quantize(last4[:], LAST, 2 * PAIR, C)
+        products([4], range(PASSES))
+        weave(rest0, gated[:])
+        gated = gather_unit(1, FRONT, REST)
+        quantize_odd(rest0, 0, FRONT, REST)
+        finish(rest1, [0, 1])
+        finish(last56, [2, 3])
+        weave(rest1, gated[:])
+        gated = gather_unit(LAST, FRONT, PAIR)
+        quantize_odd(rest1, 1, FRONT, REST)
+        products([5, 6, 7], range(LAST))
+        weave(last56, gated[:])
+        finish(gated[:, 0, :], [4])
+
+        gated = gather_unit(LAST, S - C, C)
+        quantize(last56[:], LAST, FRONT, PAIR)
+        nc.vector.tensor_copy(*weave_views(last7, gated[:]))
+        quantize(last7[:], LAST, S - C, C)
+        products([5, 6, 7], [LAST])
+        relu_rest = [keep.tile([P, REST], F32, name="relu_rest%d" % h) for h in range(HALVES)]
+        relu2(relu_rest[0][:, 0:PAIR], [5, 6], 0)
+        relu7 = relu_rest[0][:, PAIR:REST]
+        nc.vector.tensor_scalar(relu7, acc(E - 1, 0), bias[:, 0, E - 1:E], 0.0, ALU.add, ALU.max)
+        nc.vector.tensor_tensor(y[0][:, S - C:S], relu7, relu7, ALU.mult)
+        relu2(relu_rest[1][:], [5, 6, 7], 1)
+
+        first = [keep.tile([P, T], F32, name="first%d" % h) for h in range(HALVES)]
         both = [keep.tile([P, T], F32, name="both%d" % h) for h in range(HALVES)]
         for h in range(HALVES):
-            nc.vector.tensor_copy(one[h][:], y[h][:].indirect(pos1_t[:]))
-        for h, t0, t1 in ((0, 0, T), (1, 0, T - C), (1, T - C, T)):
-            nc.vector.tensor_tensor(both[h][:, t0:t1], y[h][:].indirect(pos2_t[:, t0 // 16:t1 // 16]), one[h][:, t0:t1], ALU.add)
+            nc.vector.tensor_copy(first[h][:], y[h][:].indirect(pos1_t[:]))
+        for h, t0, t1 in ((0, 0, T), (1, 0, T - P), (1, T - P, T)):
+            second = y[h][:].indirect(pos2_t[:, t0 // STRIPE:t1 // STRIPE])
+            nc.vector.tensor_tensor(both[h][:, t0:t1], second, first[h][:, t0:t1], ALU.add)
             nc.sync.dma_start(out=out[h * P:(h + 1) * P, t0:t1], in_=both[h][:, t0:t1])

@@ -34,7 +34,6 @@ def tile_moe_pre_lin_relu2_kernel(tc, xT, w_words, w_scales, b, gate, offs, pos1
     nc = tc.nc
     with ExitStack() as ctx:
         keep = ctx.enter_context(tc.tile_pool(name="keep", bufs=1))
-        ring = ctx.enter_context(tc.tile_pool(name="ring", bufs=2))
         psum = ctx.enter_context(tc.psum_pool(name="psum", bufs=1))
 
         offs_t = keep.tile([P, S // STRIPE], U16, name="offs_t")
@@ -79,8 +78,11 @@ def tile_moe_pre_lin_relu2_kernel(tc, xT, w_words, w_scales, b, gate, offs, pos1
             window = planes[a][j][:].indirect(offs_t[:, s0 // STRIPE:s1 // STRIPE])
             nc.vector.tensor_tensor(dst, window, gate_t[:, s0:s1], ALU.mult)
 
-        def gather_unit(a, s0, n):
-            gated = ring.tile([P, PACK, n], F32, name="gated")
+        room = PACK * FRONT
+        rooms = keep.tile([P, 2 * room], F32, name="rooms")
+
+        def gather_unit(a, s0, n, at):
+            gated = rooms[:, at:at + PACK * n].rearrange("p (j s) -> p j s", j=PACK)
             for j in range(PACK):
                 if (a, j, s0) == (0, 0, 0):
                     gather(gated[:, j, 0:PAIR], a, j, 0, PAIR)
@@ -113,13 +115,14 @@ def tile_moe_pre_lin_relu2_kernel(tc, xT, w_words, w_scales, b, gate, offs, pos1
             quantize(woven[:, 0:2 * (n - C)], a, s0, n - C)
             quantize(woven[:, 2 * (n - C):2 * n], a, s0 + n - C, C)
 
-        banks = [psum.tile([P, 4, C], F32, name="bank%d" % i) for i in range(8)]
-        rest_bank = {(5, 0): 3, (6, 0): 4, (5, 1): 5, (6, 1): 0, (7, 0): 6, (7, 1): 7}
+        banks = [psum.tile([P, HALVES, C], F32, name="bank%d" % i) for i in range(8)]
 
         def acc(e, h):
-            if (e, h) in rest_bank:
-                return banks[rest_bank[(e, h)]][:, 0, :]
-            return banks[e // 2][:, 2 * h + e % 2, :]
+            if e < 4:
+                return banks[4 * (e // 2) + 2 * h + e % 2][:, 0, :]
+            if e == 4:
+                return banks[0][:, h, :]
+            return banks[1 + 3 * h + e - 5][:, 0, :]
 
         def products(experts, passes):
             for h in range(HALVES):
@@ -151,50 +154,51 @@ def tile_moe_pre_lin_relu2_kernel(tc, xT, w_words, w_scales, b, gate, offs, pos1
         rest0, rest1 = woven_tile(0, FRONT, REST), woven_tile(1, FRONT, REST)
         last56, last7 = woven_tile(LAST, FRONT, PAIR), woven_tile(LAST, S - C, C)
 
-        gated = gather_unit(0, 0, FRONT)
-        weave(front0, gated[:])
-        gated = gather_unit(1, 0, FRONT)
+        gated = gather_unit(0, 0, FRONT, 0)
+        weave(front0, gated)
+        gated = gather_unit(1, 0, FRONT, room)
         quantize_odd(front0, 0, 0, FRONT)
-        weave(front1, gated[:])
-        gated = gather_unit(LAST, 0, FRONT)
+        weave(front1, gated)
+        gated = gather_unit(LAST, 0, FRONT, 0)
         quantize_odd(front1, 1, 0, FRONT)
+        products([0, 1, 2, 3], range(LAST))
         weave(last01, gated[:, :, 0:PAIR])
         weave(last23, gated[:, :, PAIR:2 * PAIR])
         weave(last4, gated[:, :, 2 * PAIR:FRONT])
         quantize(last01[:], LAST, 0, PAIR)
-        products([0, 1], range(PASSES))
+        products([0, 1], [LAST])
 
-        gated = gather_unit(0, FRONT, REST)
+        gated = gather_unit(0, FRONT, REST, room)
         quantize(last23[:], LAST, PAIR, PAIR)
-        products([2, 3], range(PASSES))
+        products([2, 3], [LAST])
         quantize(last4[:], LAST, 2 * PAIR, C)
-        products([4], range(PASSES))
-        weave(rest0, gated[:])
-        gated = gather_unit(1, FRONT, REST)
+        weave(rest0, gated)
+        gated = gather_unit(1, FRONT, REST, room - PACK * REST)
         quantize_odd(rest0, 0, FRONT, REST)
         finish(rest1, [0, 1])
+        products([4], range(PASSES))
         finish(last56, [2, 3])
-        weave(rest1, gated[:])
-        gated = gather_unit(LAST, FRONT, PAIR)
+        weave(rest1, gated)
+        gated = gather_unit(LAST, FRONT, PAIR, room)
         quantize_odd(rest1, 1, FRONT, REST)
         products([5, 6, 7], range(LAST))
-        weave(last56, gated[:])
-        finish(gated[:, 0, :], [4])
+        weave(last56, gated)
+        finish(gated[:, PACK - 1, :], [4])
 
-        gated = gather_unit(LAST, S - C, C)
+        gated = gather_unit(LAST, S - C, C, room - (PACK - 1) * C)
         quantize(last56[:], LAST, FRONT, PAIR)
-        nc.vector.tensor_copy(*weave_views(last7, gated[:]))
+        nc.vector.tensor_copy(*weave_views(last7, gated))
         quantize(last7[:], LAST, S - C, C)
         products([5, 6, 7], [LAST])
-        relu_rest = [keep.tile([P, REST], F32, name="relu_rest%d" % h) for h in range(HALVES)]
-        relu2(relu_rest[0][:, 0:PAIR], [5, 6], 0)
-        relu7 = relu_rest[0][:, PAIR:REST]
-        nc.vector.tensor_scalar(relu7, acc(E - 1, 0), bias[:, 0, E - 1:E], 0.0, ALU.add, ALU.max)
-        nc.vector.tensor_tensor(y[0][:, S - C:S], relu7, relu7, ALU.mult)
-        relu2(relu_rest[1][:], [5, 6, 7], 1)
-
         first = [keep.tile([P, T], F32, name="first%d" % h) for h in range(HALVES)]
         both = [keep.tile([P, T], F32, name="both%d" % h) for h in range(HALVES)]
+        relu_rest = keep.tile([P, REST], F32, name="relu_rest")
+        relu2(relu_rest[:, 0:PAIR], [5, 6], 0)
+        relu7 = relu_rest[:, PAIR:REST]
+        nc.vector.tensor_scalar(relu7, acc(E - 1, 0), bias[:, 0, E - 1:E], 0.0, ALU.add, ALU.max)
+        nc.vector.tensor_tensor(y[0][:, S - C:S], relu7, relu7, ALU.mult)
+        relu2(both[0][:, 0:REST], [5, 6, 7], 1)
+
         for h in range(HALVES):
             nc.vector.tensor_copy(first[h][:], y[h][:].indirect(pos1_t[:]))
         for h, t0, t1 in ((0, 0, T), (1, 0, T - P), (1, T - P, T)):

from contextlib import ExitStack

import concourse.mybir as mybir

K, T, E, C, N = 1536, 512, 8, 128, 256
S = E * C
FLOPS = 2 * K * N * S
BYTES = 4 * K * T + E * K * N // 2 + E * K * N // 32 + 4 * N * E + 4 * S + 2 * 128 * (S + 2 * T) // 16 + 4 * N * T

F32 = mybir.dt.float32
BF16 = mybir.dt.bfloat16
I32 = mybir.dt.int32
U32 = mybir.dt.uint32
U16 = mybir.dt.uint16
U8 = mybir.dt.uint8
FP8X4 = mybir.dt.float8_e4m3fn_x4
FP4X4 = mybir.dt.float4_e2m1fn_x4
ALU = mybir.AluOpType
ACT = mybir.ActivationFunctionType

P = 128
PACK = 4
PASSES = K // (P * PACK)
LAST = PASSES - 1
HALVES = N // P
STRIPE = 16
PAIR = 2 * C
FRONT = 5 * C
REST = S - FRONT
WINDOW = FRONT + 32


def tile_moe_pre_lin_relu2_kernel(tc, xT, w_words, w_scales, b, gate, offs, pos1, pos2, out):
    nc = tc.nc
    with ExitStack() as ctx:
        keep = ctx.enter_context(tc.tile_pool(name="keep", bufs=1))
        psum = ctx.enter_context(tc.psum_pool(name="psum", bufs=1))

        offs_t = keep.tile([P, S // STRIPE], U16, name="offs_t")
        pos1_t = keep.tile([P, T // STRIPE], U16, name="pos1_t")
        pos2_t = keep.tile([P, T // STRIPE], U16, name="pos2_t")
        gate_t = keep.tile([P, S], F32, name="gate_t")
        planes = [[keep.tile([P, WINDOW], F32, name="plane%d%d" % (a, j)) for j in range(PACK)] for a in range(PASSES)]
        w_scale_t = keep.tile([P, E * PASSES, N], U8, name="w_scale_t", align_bytes=64)
        w_word_t = [keep.tile([P, 2 * PASSES, 2 * N], U8, name="w_word_t%d" % g, align_bytes=64) for g in range(E // 2)]
        bias = keep.tile([P, HALVES, E], F32, name="bias")
        y = [keep.tile([P, S], F32, name="y%d" % h) for h in range(HALVES)]

        def load_plane(a, j):
            rows = xT[a * P * PACK:(a + 1) * P * PACK, :].rearrange("(p j) t -> p j t", j=PACK)
            nc.sync.dma_start(out=planes[a][j][:, 0:T], in_=rows[:, j, :])

        def load_gate(queue, s0, s1):
            queue.dma_start(out=gate_t[:, s0:s1], in_=gate[0:P, s0:s1])

        nc.gpsimd.memset(w_scale_t[:].rearrange("p g n -> p (g n)").bitcast(I32), 0)

        load_gate(nc.scalar, 0, PAIR)
        load_plane(0, 0)
        nc.sync.dma_start(offs_t[:], offs)
        load_gate(nc.sync, PAIR, FRONT)
        for a in range(PASSES):
            for j in range(PACK):
                if (a, j) != (0, 0):
                    load_plane(a, j)
        load_gate(nc.sync, FRONT, S)
        scale_rows = w_scales.bitcast(I32).rearrange("e a q n -> q (e a) n")
        for quad in range(4):
            nc.sync.dma_start(out=w_scale_t[32 * quad:32 * quad + 4, :, :].bitcast(I32), in_=scale_rows[4 * quad:4 * quad + 4])
        word_rows = w_words.bitcast(I32).rearrange("e a p n -> p (e a) n")
        for g in range(E // 2):
            nc.sync.dma_start(out=w_word_t[g][:].bitcast(I32), in_=word_rows[:, 2 * PASSES * g:2 * PASSES * (g + 1), :])
        nc.sync.dma_start(out=bias[:], in_=b.rearrange("(h p) e -> p h e", p=P))
        nc.sync.dma_start(pos1_t[:], pos1)
        nc.sync.dma_start(pos2_t[:], pos2)

        def gather(dst, a, j, s0, s1):
            window = planes[a][j][:].indirect(offs_t[:, s0 // STRIPE:s1 // STRIPE])
            nc.vector.tensor_tensor(dst, window, gate_t[:, s0:s1], ALU.mult)

        room = PACK * FRONT
        rooms = keep.tile([P, 2 * room], F32, name="rooms")

        def gather_unit(a, s0, n, at):
            gated = rooms[:, at:at + PACK * n].rearrange("p (j s) -> p j s", j=PACK)
            for j in range(PACK):
                if (a, j, s0) == (0, 0, 0):
                    gather(gated[:, j, 0:PAIR], a, j, 0, PAIR)
                    gather(gated[:, j, PAIR:n], a, j, PAIR, n)
                else:
                    gather(gated[:, j, :], a, j, s0, s0 + n)
            return gated

        def woven_tile(a, s0, n):
            return keep.tile([P, 2 * n], F32, name="woven%d_%d" % (a, s0), align_bytes=64)

        def weave_views(woven, gated):
            dst = woven[:].bitcast(BF16).rearrange("p (c i j) -> p c j i", i=4, j=PACK)
            return dst, gated.rearrange("p j (c i) -> p c j i", i=4)

        def weave(woven, gated):
            nc.scalar.activation(*weave_views(woven, gated), ACT.Copy)

        codes = {}

        def quantize(woven, a, s0, n):
            words = keep.tile([P, n], U32, name="x_words%d_%d" % (a, s0), align_bytes=64)
            scales = keep.tile([P, n], U8, name="x_scales%d_%d" % (a, s0), align_bytes=64)
            nc.vector.quantize_mx(out=words[:].bitcast(FP8X4), scales=scales[:], in_=woven.bitcast(BF16))
            for e in range(s0 // C, (s0 + n) // C):
                c0 = e * C - s0
                codes[(a, e)] = (words[:, c0:c0 + C], scales[:, c0:c0 + C])

        def quantize_odd(woven, a, s0, n):
            quantize(woven[:, 0:2 * (n - C)], a, s0, n - C)
            quantize(woven[:, 2 * (n - C):2 * n], a, s0 + n - C, C)

        banks = [psum.tile([P, HALVES, C], F32, name="bank%d" % i) for i in range(8)]

        def acc(e, h):
            if e < 4:
                return banks[4 * (e // 2) + 2 * h + e % 2][:, 0, :]
            if e == 4:
                return banks[0][:, h, :]
            return banks[1 + 3 * h + e - 5][:, 0, :]

        def products(experts, passes):
            for h in range(HALVES):
                for e in experts:
                    for a in passes:
                        words, scales = codes[(a, e)]
                        nc.tensor.matmul_mx(
                            out=acc(e, h),
                            lhsT=w_word_t[e // 2][:, (e % 2) * PASSES + a, 2 * P * h:2 * P * (h + 1)].bitcast(FP4X4),
                            lhsT_scale=w_scale_t[:, e * PASSES + a, P * h:P * (h + 1)],
                            rhs=words.bitcast(FP8X4),
                            rhs_scale=scales,
                            start=(a == 0),
                            stop=(a == LAST),
                        )

        def relu2(buf, experts, h):
            for i, e in enumerate(experts):
                nc.scalar.activation(buf[:, i * C:(i + 1) * C], acc(e, h), ACT.Relu, bias=bias[:, h, e:e + 1])
            nc.scalar.activation(y[h][:, experts[0] * C:(experts[-1] + 1) * C], buf, ACT.Square)

        def finish(buf, experts):
            n = len(experts) * C
            for h in range(HALVES):
                relu2(buf[:, h * n:(h + 1) * n], experts, h)

        front0, front1 = woven_tile(0, 0, FRONT), woven_tile(1, 0, FRONT)
        last01, last23, last4 = woven_tile(LAST, 0, PAIR), woven_tile(LAST, PAIR, PAIR), woven_tile(LAST, 2 * PAIR, C)
        rest0, rest1 = woven_tile(0, FRONT, REST), woven_tile(1, FRONT, REST)
        last56, last7 = woven_tile(LAST, FRONT, PAIR), woven_tile(LAST, S - C, C)

        gated = gather_unit(0, 0, FRONT, 0)
        weave(front0, gated)
        gated = gather_unit(1, 0, FRONT, room)
        quantize_odd(front0, 0, 0, FRONT)
        weave(front1, gated)
        gated = gather_unit(LAST, 0, FRONT, 0)
        quantize_odd(front1, 1, 0, FRONT)
        products([0, 1, 2, 3], range(LAST))
        weave(last01, gated[:, :, 0:PAIR])
        weave(last23, gated[:, :, PAIR:2 * PAIR])
        weave(last4, gated[:, :, 2 * PAIR:FRONT])
        quantize(last01[:], LAST, 0, PAIR)
        products([0, 1], [LAST])

        gated = gather_unit(0, FRONT, REST, room)
        quantize(last23[:], LAST, PAIR, PAIR)
        products([2, 3], [LAST])
        quantize(last4[:], LAST, 2 * PAIR, C)
        weave(rest0, gated)
        gated = gather_unit(1, FRONT, REST, room - PACK * REST)
        quantize_odd(rest0, 0, FRONT, REST)
        finish(rest1, [0, 1])
        products([4], range(PASSES))
        finish(last56, [2, 3])
        weave(rest1, gated)
        gated = gather_unit(LAST, FRONT, PAIR, room)
        quantize_odd(rest1, 1, FRONT, REST)
        products([5, 6, 7], range(LAST))
        weave(last56, gated)
        finish(gated[:, PACK - 1, :], [4])

        gated = gather_unit(LAST, S - C, C, room - (PACK - 1) * C)
        quantize(last56[:], LAST, FRONT, PAIR)
        nc.vector.tensor_copy(*weave_views(last7, gated))
        quantize(last7[:], LAST, S - C, C)
        products([5, 6, 7], [LAST])
        first = [keep.tile([P, T], F32, name="first%d" % h) for h in range(HALVES)]
        both = [keep.tile([P, T], F32, name="both%d" % h) for h in range(HALVES)]
        relu_rest = keep.tile([P, REST], F32, name="relu_rest")
        relu2(relu_rest[:, 0:PAIR], [5, 6], 0)
        relu7 = relu_rest[:, PAIR:REST]
        nc.vector.tensor_scalar(relu7, acc(E - 1, 0), bias[:, 0, E - 1:E], 0.0, ALU.add, ALU.max)
        nc.vector.tensor_tensor(y[0][:, S - C:S], relu7, relu7, ALU.mult)
        relu2(both[0][:, 0:REST], [5, 6, 7], 1)

        for h in range(HALVES):
            nc.vector.tensor_copy(first[h][:], y[h][:].indirect(pos1_t[:]))
        for h, t0, t1 in ((0, 0, T), (1, 0, T - P), (1, T - P, T)):
            second = y[h][:].indirect(pos2_t[:, t0 // STRIPE:t1 // STRIPE])
            nc.vector.tensor_tensor(both[h][:, t0:t1], second, first[h][:, t0:t1], ALU.add)
            nc.sync.dma_start(out=out[h * P:(h + 1) * P, t0:t1], in_=both[h][:, t0:t1])
